import numpy as np, ml_dtypes
CORES = [24,25,26,27,28,29,30,31,152,153,154,155,156,157,158,159]
N = 16
ROOT = 11
def setup_inputs(rng):
    return {"x": rng.standard_normal((N, 128, 8), dtype=np.float32).astype(ml_dtypes.bfloat16)}
def reference(x):
    return {"y": np.broadcast_to(x[ROOT], x.shape)}

from concourse.bass import DstId, RemoteDMATransfer

SCRATCH = {
    "buf": ("dram", [128, 8], "bfloat16"),
}
SEMAPHORES = ["loaded", "sent", "arrived", "stored"]


def rank_program(g, core, T, topo):
    if T.rank_of(core) is None:
        return
    root = T.cores[T.root]

    if core != root:
        g.sync.wait_ge(T.sem.arrived, 1)
        g.sync.dma_start(T.y[:], T.buf[:]).then_inc(T.sem.stored, 16)
        g.wait_ge(T.sem.stored, 16)
        return

    g.sync.dma_start(T.buf[:], T.x[:]).then_inc(T.sem.loaded, 16)
    g.scalar.dma_start(T.y[:], T.x[:]).then_inc(T.sem.stored, 16)

    others = [c for c in T.cores if c != root]
    same_chip = lambda c: (topo.host(c), topo.chip(c)) == (topo.host(root), topo.chip(root))
    far = [c for c in others if not same_chip(c)]
    near = [c for c in others if same_chip(c)]
    transfers = []
    for engine, dst in list(enumerate(far)) + list(enumerate(near, start=8)):
        rid, pid = topo.addr(dst, root)
        transfers.append(RemoteDMATransfer(
            dst_ids=[DstId(rid=rid, pnc=pid)], dma_engine_mask=1 << engine, remote_sem=T.sem.arrived,
            src=T.buf[:], dst=T.buf[:]))

    g.wait_ge(T.sem.loaded, 16)
    g.remote_dma_fused(transfers, local_sem=T.sem.sent)
    g.wait_ge(T.sem.sent, len(transfers))
    g.wait_ge(T.sem.stored, 16)
